import numpy as np
import ml_dtypes

BF16 = ml_dtypes.bfloat16


def bf(x):
    return np.asarray(x, np.float32).astype(BF16)


def f32(x):
    return np.asarray(x, np.float32)


def f64(x):
    return np.asarray(x).astype(np.float64)


def striped(idx):
    return np.tile(idx.reshape(-1, 16).T, (8, 1))


def rows(idx, k):
    return np.tile(idx, (k, 1))


def look(tab, idx):
    return np.take_along_axis(f64(tab), rows(idx, len(tab)), axis=1)


K, S, V, N, M = 512, 2048, 1024, 1024, 256


def silu(v):
    return v / (1.0 + np.exp(-v))


def setup_inputs():
    return {"tab": f32(np.random.standard_normal((2, K, S))), "y": f32(np.random.standard_normal((K, V))), "w": bf(np.random.standard_normal((K, M)) / np.sqrt(K)), "b": f32(0.5 * np.random.standard_normal((M, 1))), "offs": striped(np.random.permutation(S)[:N])}


def reference(tab, y, w, b, offs):
    idx = offs[:16].T.reshape(-1)
    x = (look(tab[0], idx) - f64(y)) * (silu(look(tab[1], idx)))
    return np.maximum(f64(w).T @ x + f64(b), 0.0)

@@ -1,0 +1,73 @@
+import concourse.mybir as mybir
+
+BF16, F32, U16 = mybir.dt.bfloat16, mybir.dt.float32, mybir.dt.uint16
+ALU = mybir.AluOpType
+FUNC = mybir.ActivationFunctionType
+
+P = 128
+ROWS, PLACES, PICKS, OUTS = 512, 2048, 1024, 256
+ROW_BLOCKS = ROWS // P
+OUT_BLOCKS = OUTS // P
+PIECE = 512
+PIECES = PICKS // PIECE
+LIST_COLUMNS = PIECE // 16
+
+FLOPS = 2 * ROWS * OUTS * PICKS
+
+
+def tile_lookup_vg_subsilu_relu_kernel(tc, tab, y, w, b, offs, out):
+    nc = tc.nc
+    with (
+        tc.tile_pool(name="held", bufs=1) as held,
+        tc.tile_pool(name="windows", bufs=ROW_BLOCKS) as windows,
+        tc.tile_pool(name="pieces", bufs=ROW_BLOCKS * PIECES) as pieces,
+        tc.tile_pool(name="results", bufs=OUT_BLOCKS * PIECES) as results,
+        tc.psum_pool(name="psum", bufs=1) as psum,
+    ):
+        offsets = held.tile([P, PICKS // 16], U16, name="offsets")
+        nc.sync.dma_start(offsets[:], offs)
+        weights = held.tile([P, ROW_BLOCKS, OUTS], BF16, name="weights")
+        biases = [held.tile([P, 1], F32, name=f"bias{m}") for m in range(OUT_BLOCKS)]
+        sums = [[psum.tile([P, PIECE], F32, name=f"sum{m}_{h}") for h in range(PIECES)] for m in range(OUT_BLOCKS)]
+
+        for k in range(ROW_BLOCKS):
+            rows = slice(k * P, (k + 1) * P)
+            gates = windows.tile([P, PLACES], F32, name="gates")
+            values = windows.tile([P, PLACES], F32, name="values")
+            nc.sync.dma_start(gates[:], tab[1, rows, :])
+            nc.sync.dma_start(values[:], tab[0, rows, :])
+            streams = []
+            for h in range(PIECES):
+                stream = pieces.tile([P, PIECE], F32, name="stream")
+                nc.sync.dma_start(stream[:], y[rows, h * PIECE : (h + 1) * PIECE])
+                streams.append(stream)
+            if k == 0:
+                nc.sync.dma_start(weights[:], w.rearrange("(k p) m -> p k m", p=P))
+                for m in range(OUT_BLOCKS):
+                    nc.sync.dma_start(biases[m][:], b[m * P : (m + 1) * P, :])
+
+            for h in range(PIECES):
+                picks = offsets[:, h * LIST_COLUMNS : (h + 1) * LIST_COLUMNS]
+                gate = pieces.tile([P, PIECE], F32, name="gate")
+                nc.scalar.activation(gate[:], gates[:].indirect(picks), FUNC.Silu)
+                difference = pieces.tile([P, PIECE], F32, name="difference")
+                nc.vector.tensor_tensor(difference[:], values[:].indirect(picks), streams[h][:], ALU.subtract)
+                x = pieces.tile([P, PIECE], BF16, name="x")
+                nc.vector.tensor_tensor(x[:], difference[:], gate[:], ALU.mult)
+                for m in range(OUT_BLOCKS):
+                    nc.tensor.matmul(
+                        sums[m][h][:],
+                        weights[:, k, m * P : (m + 1) * P],
+                        x[:],
+                        start=(k == 0),
+                        stop=(k == ROW_BLOCKS - 1),
+                    )
+
+        for h in range(PIECES):
+            for m in range(OUT_BLOCKS):
+                result = results.tile([P, PIECE], F32, name="result")
+                if h < PIECES - 1 or m == 0:
+                    nc.scalar.activation(result[:], sums[m][h][:], FUNC.Relu, bias=biases[m][:])
+                else:
+                    nc.vector.tensor_scalar(result[:], sums[m][h][:], biases[m][:], 0.0, ALU.add, ALU.max)
+                nc.sync.dma_start(out[m * P : (m + 1) * P, h * PIECE : (h + 1) * PIECE], result[:])

@@ -30,28 +30,28 @@ def tile_lookup_vg_subsilu_relu_kernel(tc, tab, y, w, b, offs, out):
         biases = [held.tile([P, 1], F32, name=f"bias{m}") for m in range(OUT_BLOCKS)]
         sums = [[psum.tile([P, PIECE], F32, name=f"sum{m}_{h}") for h in range(PIECES)] for m in range(OUT_BLOCKS)]
 
+        tab_rows = tab.rearrange("t (p k) s -> t k p s", k=ROW_BLOCKS)
+        y_rows = y.rearrange("(p k) v -> k p v", k=ROW_BLOCKS)
+        w_rows = w.rearrange("(p k) m -> p k m", k=ROW_BLOCKS)
         for k in range(ROW_BLOCKS):
-            rows = slice(k * P, (k + 1) * P)
-            gates = windows.tile([P, PLACES], F32, name="gates")
             values = windows.tile([P, PLACES], F32, name="values")
-            nc.sync.dma_start(gates[:], tab[1, rows, :])
-            nc.sync.dma_start(values[:], tab[0, rows, :])
-            streams = []
-            for h in range(PIECES):
-                stream = pieces.tile([P, PIECE], F32, name="stream")
-                nc.sync.dma_start(stream[:], y[rows, h * PIECE : (h + 1) * PIECE])
-                streams.append(stream)
+            nc.sync.dma_start(values[:], tab_rows[0, k])
+            stream = windows.tile([P, PICKS], F32, name="stream")
+            nc.sync.dma_start(stream[:], y_rows[k])
+            gates = windows.tile([P, PLACES], F32, name="gates")
+            nc.sync.dma_start(gates[:], tab_rows[1, k])
             if k == 0:
-                nc.sync.dma_start(weights[:], w.rearrange("(k p) m -> p k m", p=P))
+                nc.sync.dma_start(weights[:], w_rows)
                 for m in range(OUT_BLOCKS):
                     nc.sync.dma_start(biases[m][:], b[m * P : (m + 1) * P, :])
 
             for h in range(PIECES):
+                columns = slice(h * PIECE, (h + 1) * PIECE)
                 picks = offsets[:, h * LIST_COLUMNS : (h + 1) * LIST_COLUMNS]
+                difference = pieces.tile([P, PIECE], F32, name="difference")
+                nc.vector.tensor_tensor(difference[:], values[:].indirect(picks), stream[:, columns], ALU.subtract)
                 gate = pieces.tile([P, PIECE], F32, name="gate")
                 nc.scalar.activation(gate[:], gates[:].indirect(picks), FUNC.Silu)
-                difference = pieces.tile([P, PIECE], F32, name="difference")
-                nc.vector.tensor_tensor(difference[:], values[:].indirect(picks), streams[h][:], ALU.subtract)
                 x = pieces.tile([P, PIECE], BF16, name="x")
                 nc.vector.tensor_tensor(x[:], difference[:], gate[:], ALU.mult)
                 for m in range(OUT_BLOCKS):
@@ -66,7 +66,7 @@ def tile_lookup_vg_subsilu_relu_kernel(tc, tab, y, w, b, offs, out):
         for h in range(PIECES):
             for m in range(OUT_BLOCKS):
                 result = results.tile([P, PIECE], F32, name="result")
-                if h < PIECES - 1 or m == 0:
+                if m % 2 == 0:
                     nc.scalar.activation(result[:], sums[m][h][:], FUNC.Relu, bias=biases[m][:])
                 else:
                     nc.vector.tensor_scalar(result[:], sums[m][h][:], biases[m][:], 0.0, ALU.add, ALU.max)

@@ -11,6 +11,8 @@ OUT_BLOCKS = OUTS // P
 PIECE = 512
 PIECES = PICKS // PIECE
 LIST_COLUMNS = PIECE // 16
+SLICE = PIECE // 2
+SLICES = PICKS // SLICE
 
 FLOPS = 2 * ROWS * OUTS * PICKS
 
@@ -21,53 +23,60 @@ def tile_lookup_vg_subsilu_relu_kernel(tc, tab, y, w, b, offs, out):
         tc.tile_pool(name="held", bufs=1) as held,
         tc.tile_pool(name="windows", bufs=ROW_BLOCKS) as windows,
         tc.tile_pool(name="pieces", bufs=ROW_BLOCKS * PIECES) as pieces,
-        tc.tile_pool(name="results", bufs=OUT_BLOCKS * PIECES) as results,
+        tc.tile_pool(name="slices", bufs=ROW_BLOCKS * SLICES) as slices,
+        tc.tile_pool(name="results", bufs=OUT_BLOCKS * SLICES) as results,
         tc.psum_pool(name="psum", bufs=1) as psum,
     ):
         offsets = held.tile([P, PICKS // 16], U16, name="offsets")
         nc.sync.dma_start(offsets[:], offs)
-        weights = held.tile([P, ROW_BLOCKS, OUTS], BF16, name="weights")
         biases = [held.tile([P, 1], F32, name=f"bias{m}") for m in range(OUT_BLOCKS)]
-        sums = [[psum.tile([P, PIECE], F32, name=f"sum{m}_{h}") for h in range(PIECES)] for m in range(OUT_BLOCKS)]
+        for m in range(OUT_BLOCKS):
+            nc.scalar.dma_start(biases[m][:], b[m * P : (m + 1) * P, :])
+        weights = held.tile([P, ROW_BLOCKS, OUTS], BF16, name="weights")
+        sums = [[psum.tile([P, SLICE], F32, name=f"sum{m}_{q}") for q in range(SLICES)] for m in range(OUT_BLOCKS)]
 
         tab_rows = tab.rearrange("t (p k) s -> t k p s", k=ROW_BLOCKS)
         y_rows = y.rearrange("(p k) v -> k p v", k=ROW_BLOCKS)
         w_rows = w.rearrange("(p k) m -> p k m", k=ROW_BLOCKS)
         for k in range(ROW_BLOCKS):
             values = windows.tile([P, PLACES], F32, name="values")
-            nc.sync.dma_start(values[:], tab_rows[0, k])
-            stream = windows.tile([P, PICKS], F32, name="stream")
-            nc.sync.dma_start(stream[:], y_rows[k])
             gates = windows.tile([P, PLACES], F32, name="gates")
+            streams = [pieces.tile([P, PIECE], F32, name="stream") for h in range(PIECES)]
+            nc.sync.dma_start(values[:], tab_rows[0, k])
+            nc.sync.dma_start(streams[0][:], y_rows[k, :, 0:PIECE])
             nc.sync.dma_start(gates[:], tab_rows[1, k])
+            nc.sync.dma_start(streams[1][:], y_rows[k, :, PIECE : 2 * PIECE])
             if k == 0:
                 nc.sync.dma_start(weights[:], w_rows)
-                for m in range(OUT_BLOCKS):
-                    nc.sync.dma_start(biases[m][:], b[m * P : (m + 1) * P, :])
 
+            differences, looked_up_gates = [], []
             for h in range(PIECES):
-                columns = slice(h * PIECE, (h + 1) * PIECE)
                 picks = offsets[:, h * LIST_COLUMNS : (h + 1) * LIST_COLUMNS]
                 difference = pieces.tile([P, PIECE], F32, name="difference")
-                nc.vector.tensor_tensor(difference[:], values[:].indirect(picks), stream[:, columns], ALU.subtract)
+                nc.vector.tensor_tensor(difference[:], values[:].indirect(picks), streams[h][:], ALU.subtract)
+                differences.append(difference)
                 gate = pieces.tile([P, PIECE], F32, name="gate")
                 nc.scalar.activation(gate[:], gates[:].indirect(picks), FUNC.Silu)
-                x = pieces.tile([P, PIECE], BF16, name="x")
-                nc.vector.tensor_tensor(x[:], difference[:], gate[:], ALU.mult)
+                looked_up_gates.append(gate)
+            for q in range(SLICES):
+                h, start = divmod(q * SLICE, PIECE)
+                columns = slice(start, start + SLICE)
+                x = slices.tile([P, SLICE], BF16, name="x")
+                nc.vector.tensor_tensor(x[:], differences[h][:, columns], looked_up_gates[h][:, columns], ALU.mult)
                 for m in range(OUT_BLOCKS):
                     nc.tensor.matmul(
-                        sums[m][h][:],
+                        sums[m][q][:],
                         weights[:, k, m * P : (m + 1) * P],
                         x[:],
                         start=(k == 0),
                         stop=(k == ROW_BLOCKS - 1),
                     )
 
-        for h in range(PIECES):
+        for q in range(SLICES):
             for m in range(OUT_BLOCKS):
-                result = results.tile([P, PIECE], F32, name="result")
+                result = results.tile([P, SLICE], F32, name="result")
                 if m % 2 == 0:
-                    nc.scalar.activation(result[:], sums[m][h][:], FUNC.Relu, bias=biases[m][:])
+                    nc.scalar.activation(result[:], sums[m][q][:], FUNC.Relu, bias=biases[m][:])
                 else:
-                    nc.vector.tensor_scalar(result[:], sums[m][h][:], biases[m][:], 0.0, ALU.add, ALU.max)
-                nc.sync.dma_start(out[m * P : (m + 1) * P, h * PIECE : (h + 1) * PIECE], result[:])
+                    nc.vector.tensor_scalar(result[:], sums[m][q][:], biases[m][:], 0.0, ALU.add, ALU.max)
+                nc.sync.dma_start(out[m * P : (m + 1) * P, q * SLICE : (q + 1) * SLICE], result[:])

import concourse.mybir as mybir

BF16, F32, U16 = mybir.dt.bfloat16, mybir.dt.float32, mybir.dt.uint16
ALU = mybir.AluOpType
FUNC = mybir.ActivationFunctionType

P = 128
ROWS, PLACES, PICKS, OUTS = 512, 2048, 1024, 256
ROW_BLOCKS = ROWS // P
OUT_BLOCKS = OUTS // P
PIECE = 512
PIECES = PICKS // PIECE
LIST_COLUMNS = PIECE // 16
SLICE = PIECE // 2
SLICES = PICKS // SLICE

FLOPS = 2 * ROWS * OUTS * PICKS


def tile_lookup_vg_subsilu_relu_kernel(tc, tab, y, w, b, offs, out):
    nc = tc.nc
    with (
        tc.tile_pool(name="held", bufs=1) as held,
        tc.tile_pool(name="windows", bufs=ROW_BLOCKS) as windows,
        tc.tile_pool(name="pieces", bufs=ROW_BLOCKS * PIECES) as pieces,
        tc.tile_pool(name="slices", bufs=ROW_BLOCKS * SLICES) as slices,
        tc.tile_pool(name="results", bufs=OUT_BLOCKS * SLICES) as results,
        tc.psum_pool(name="psum", bufs=1) as psum,
    ):
        offsets = held.tile([P, PICKS // 16], U16, name="offsets")
        nc.sync.dma_start(offsets[:], offs)
        biases = [held.tile([P, 1], F32, name=f"bias{m}") for m in range(OUT_BLOCKS)]
        for m in range(OUT_BLOCKS):
            nc.scalar.dma_start(biases[m][:], b[m * P : (m + 1) * P, :])
        weights = held.tile([P, ROW_BLOCKS, OUTS], BF16, name="weights")
        sums = [[psum.tile([P, SLICE], F32, name=f"sum{m}_{q}") for q in range(SLICES)] for m in range(OUT_BLOCKS)]

        tab_rows = tab.rearrange("t (p k) s -> t k p s", k=ROW_BLOCKS)
        y_rows = y.rearrange("(p k) v -> k p v", k=ROW_BLOCKS)
        w_rows = w.rearrange("(p k) m -> p k m", k=ROW_BLOCKS)
        for k in range(ROW_BLOCKS):
            values = windows.tile([P, PLACES], F32, name="values")
            gates = windows.tile([P, PLACES], F32, name="gates")
            streams = [pieces.tile([P, PIECE], F32, name="stream") for h in range(PIECES)]
            nc.sync.dma_start(values[:], tab_rows[0, k])
            nc.sync.dma_start(streams[0][:], y_rows[k, :, 0:PIECE])
            nc.sync.dma_start(gates[:], tab_rows[1, k])
            nc.sync.dma_start(streams[1][:], y_rows[k, :, PIECE : 2 * PIECE])
            if k == 0:
                nc.sync.dma_start(weights[:], w_rows)

            differences, looked_up_gates = [], []
            for h in range(PIECES):
                picks = offsets[:, h * LIST_COLUMNS : (h + 1) * LIST_COLUMNS]
                difference = pieces.tile([P, PIECE], F32, name="difference")
                nc.vector.tensor_tensor(difference[:], values[:].indirect(picks), streams[h][:], ALU.subtract)
                differences.append(difference)
                gate = pieces.tile([P, PIECE], F32, name="gate")
                nc.scalar.activation(gate[:], gates[:].indirect(picks), FUNC.Silu)
                looked_up_gates.append(gate)
            for q in range(SLICES):
                h, start = divmod(q * SLICE, PIECE)
                columns = slice(start, start + SLICE)
                x = slices.tile([P, SLICE], BF16, name="x")
                nc.vector.tensor_tensor(x[:], differences[h][:, columns], looked_up_gates[h][:, columns], ALU.mult)
                for m in range(OUT_BLOCKS):
                    nc.tensor.matmul(
                        sums[m][q][:],
                        weights[:, k, m * P : (m + 1) * P],
                        x[:],
                        start=(k == 0),
                        stop=(k == ROW_BLOCKS - 1),
                    )

        for q in range(SLICES):
            for m in range(OUT_BLOCKS):
                result = results.tile([P, SLICE], F32, name="result")
                if m % 2 == 0:
                    nc.scalar.activation(result[:], sums[m][q][:], FUNC.Relu, bias=biases[m][:])
                else:
                    nc.vector.tensor_scalar(result[:], sums[m][q][:], biases[m][:], 0.0, ALU.add, ALU.max)
                nc.sync.dma_start(out[m * P : (m + 1) * P, q * SLICE : (q + 1) * SLICE], result[:])
